import numpy as np
import ml_dtypes


def mxq(x, axis, fmt="e4m3"):
    dtype, down = {"e4m3": (ml_dtypes.float8_e4m3fn, 7), "e5m2": (ml_dtypes.float8_e5m2, 14)}[fmt]
    v = np.moveaxis(np.asarray(x, np.float32).astype(ml_dtypes.bfloat16).astype(np.float64), axis, -1)
    blocks = v.reshape(v.shape[:-1] + (-1, 32))
    amax = np.abs(blocks).max(-1, keepdims=True)
    byte = np.maximum(np.where(amax > 0, np.frexp(amax)[1] - 1 + 127, 0) - down, 1)
    scale = np.exp2(byte - 127.0)
    codes = (blocks / scale).astype(np.float32).astype(dtype).astype(np.float64)
    return np.moveaxis((codes * scale).reshape(v.shape), -1, axis)


WIDE = False


def mx_kscale(k):
    if not WIDE:
        return np.ones(k)
    levels = np.array([10, -10, 5, -5, 0])
    if k % 512:
        return np.exp2(np.random.permutation(np.resize(levels, k // 32))).repeat(32)
    a = np.empty((k // 512, 16))
    for p in range(k // 512):
        a[p, :8] = np.random.permutation(np.resize(levels, 8))
        for g in range(8):
            far = levels[np.abs(levels - a[p, g]) >= 10]
            a[p, g + 8] = far[np.random.randint(len(far))]
    return np.exp2(a.ravel()).repeat(32)


def f64(x):
    return np.asarray(x).astype(np.float64)


def striped(idx):
    return np.tile(idx.reshape(-1, 16).T, (8, 1)).astype(np.uint16)


def unstriped(offs):
    return offs[:16].T.reshape(-1).astype(np.int64)


E2M1 = np.array([0.0, 0.5, 1.0, 1.5, 2.0, 3.0, 4.0, 6.0, -0.0, -0.5, -1.0, -1.5, -2.0, -3.0, -4.0, -6.0])


def pack_weight(w, fmt):
    k, n = w.shape
    w = f64(np.asarray(w, np.float32).astype(ml_dtypes.bfloat16)).reshape(k // 32, 32, n)
    amax = np.abs(w).max(1)
    if fmt == "e4m3":
        byte = np.frexp(amax)[1] - 1 + 127 - 7
    else:
        mant, ex = np.frexp(amax / 6.0)
        byte = np.where(mant > 0.5, ex, ex - 1) + 127
    byte = np.clip(np.where(amax > 0, byte, 1), 1, 254)
    scaled = (w * np.exp2(127.0 - byte)[:, None, :]).reshape(k, n).astype(np.float32)
    by_word = np.ascontiguousarray(scaled.reshape(k // 512, 128, 4, n).transpose(0, 1, 3, 2))
    if fmt == "e4m3":
        words = by_word.astype(ml_dtypes.float8_e4m3fn).view(np.uint8)
    else:
        c = by_word.astype(ml_dtypes.float4_e2m1fn).view(np.uint8) & 0xF
        words = (c[..., 0::2] | (c[..., 1::2] << 4)).reshape(k // 512, 128, 2 * n)
    return np.ascontiguousarray(words), np.ascontiguousarray(byte.astype(np.uint8).reshape(k // 512, 16, n))


def unpack_weight(words, scales, fmt):
    g, _, n = scales.shape
    words = np.ascontiguousarray(words).reshape(g, 128, n, -1)
    if fmt == "e4m3":
        vals = words.view(ml_dtypes.float8_e4m3fn).astype(np.float64)
    else:
        nib = np.empty((g, 128, n, 4), np.uint8)
        nib[..., 0::2] = words & 0xF
        nib[..., 1::2] = words >> 4
        vals = E2M1[nib]
    vals = vals * np.repeat(np.exp2(scales.astype(np.float64) - 127.0), 8, axis=1)[..., None]
    return vals.transpose(0, 1, 3, 2).reshape(g * 512, n)


def gelu(v):
    return 0.5 * v * (1.0 + np.tanh(np.sqrt(2.0 / np.pi) * (v + 0.044715 * v**3)))


K, T, S, H, T3, S2, P = 1024, 4096, 1024, 1024, 2048, 512, 512


def setup_inputs():
    n = np.random.standard_normal
    s = mx_kscale(K)[:, None]
    u = mx_kscale(H)[:, None]
    tab_words, tab_scales = pack_weight(n((K, T)) * s, "e4m3")
    tab2_words, tab2_scales = pack_weight(n((H, T3)) / np.sqrt(H) / u, "e4m3")
    return {
        "tab_words": tab_words, "tab_scales": tab_scales,
        "offs": striped(np.random.permutation(T)[:S]),
        "tab2_words": tab2_words, "tab2_scales": tab2_scales,
        "offs2": striped(np.random.permutation(T3)[:S2]),
        "pos1": striped(np.random.permutation(S)[:P]),
        "pos2": striped(np.random.permutation(S)[:P]),
        "w1": (1.5 * n((K, H)) / np.sqrt(K) / s).astype(np.float32),
        "gain": (1.4 * np.exp(0.3 * n(H)) * u[:, 0]).astype(np.float32),
        "room": n((H, P)).astype(np.float32),
        "base": (0.6 * n(H) * u[:, 0]).astype(np.float32),
        "level": n(S2).astype(np.float32),
    }


def reference(tab_words, tab_scales, offs, tab2_words, tab2_scales, offs2, pos1, pos2, w1, gain, room, base, level):
    v = unpack_weight(tab_words, tab_scales, "e4m3")[:, unstriped(offs)]
    v2 = unpack_weight(tab2_words, tab2_scales, "e4m3")[:, unstriped(offs2)]
    h = np.tanh(mxq(f64(w1), 0, "e4m3").T @ v) * f64(gain)[:, None]
    x1 = mxq(h[:, unstriped(pos1)] * f64(room), 0, "e4m3")
    x2 = mxq(np.maximum(h[:, unstriped(pos2)], f64(base)[:, None]), 0, "e4m3")
    e1 = v2.T @ x1
    e2 = v2.T @ x2
    return e1 * e2 + np.maximum(e1, f64(level)[:, None])

@@ -1,0 +1,265 @@
+from contextlib import ExitStack
+
+import concourse.mybir as mybir
+
+K, T, S, H, T2, S2, J = 1024, 4096, 1024, 1024, 2048, 512, 512
+FLOPS = 2 * K * H * S + 2 * 2 * H * S2 * J
+
+F32 = mybir.dt.float32
+BF16 = mybir.dt.bfloat16
+I32 = mybir.dt.int32
+U32 = mybir.dt.uint32
+U16 = mybir.dt.uint16
+U8 = mybir.dt.uint8
+FP8X4 = mybir.dt.float8_e4m3fn_x4
+ACT = mybir.ActivationFunctionType
+ALU = mybir.AluOpType
+
+P = 128
+PACK = 4
+PASS = P * PACK
+BANK = 512
+CHUNK = 256
+GAIN_ON_VECTOR = (0, 1, 2)
+
+
+def tile_list_showroom_lamp_scores_kernel(
+    tc, tab_words, tab_scales, offs, tab2_words, tab2_scales, offs2, pos1, pos2, w1, gain, room, base, level, out
+):
+    nc = tc.nc
+    with ExitStack() as ctx:
+        keep = ctx.enter_context(tc.tile_pool(name="keep", bufs=1))
+        ring = ctx.enter_context(tc.tile_pool(name="ring", bufs=2))
+        psum = ctx.enter_context(tc.psum_pool(name="psum", bufs=8))
+
+        def held(shape, dtype, name):
+            return keep.tile(shape, dtype, name=name, align_bytes=64)
+
+        idx = keep.tile([P, S // 16], U16, name="idx")
+        idx2 = keep.tile([P, S2 // 16], U16, name="idx2")
+        p1 = keep.tile([P, J // 16], U16, name="p1")
+        p2 = keep.tile([P, J // 16], U16, name="p2")
+
+        tabw = [held([P, T], U32, f"tabw{a}") for a in range(2)]
+        tabs = held([P, T], U8, "tabs")
+        tab2w = [held([P, T2], U32, f"tab2w{b}") for b in range(2)]
+        tab2s = held([P, T2], U8, "tab2s")
+        vw = [[held([P, BANK], U32, f"vw{a}{n}") for n in range(2)] for a in range(2)]
+        vs = held([P, S], U8, "vs")
+        v2w = [held([P, S2], U32, f"v2w{b}") for b in range(2)]
+        v2s = held([P, S2], U8, "v2s")
+        wraw = [[held([P, PACK, PASS], F32, f"wraw{b}{a}") for a in range(2)] for b in range(2)]
+        wq = [held([P, 2 * PASS], U32, f"wq{b}") for b in range(2)]
+        ws = [held([P, 2 * PASS], U8, f"ws{b}") for b in range(2)]
+        room_t = [held([P, J], F32, f"room{s}") for s in range(8)]
+        gain_t = held([P, 2, PACK], F32, "gain_t")
+        base_t = held([P, 2, PACK], F32, "base_t")
+        level_t = held([P, 4], F32, "level_t")
+
+        def load_w(b, a):
+            rows = w1[a * PASS : (a + 1) * PASS, b * PASS : (b + 1) * PASS]
+            nc.sync.dma_start(out=wraw[b][a][:], in_=rows.rearrange("(p j) c -> p j c", j=PACK))
+
+        def load_words(dst, words):
+            nc.sync.dma_start(out=dst[:].bitcast(I32), in_=words.rearrange("p t i -> p (t i)").bitcast(I32))
+
+        def load_room(s):
+            b, t = divmod(s, PACK)
+            rows = room[b * PASS : (b + 1) * PASS, :].rearrange("(p t) j -> p t j", t=PACK)
+            nc.sync.dma_start(out=room_t[s][:], in_=rows[:, t, :])
+
+        def load_scales(dst, scales, first):
+            nc.vector.memset(dst[:].bitcast(I32), 0)
+            for q in range(4):
+                nc.sync.dma_start(
+                    out=dst[32 * q + first : 32 * q + first + 8, :].bitcast(I32),
+                    in_=scales[:, 4 * q : 4 * q + 4, :].bitcast(I32),
+                )
+
+        load_w(0, 0)
+        load_scales(tabs, tab_scales, 0)
+        nc.sync.dma_start(idx[:], offs)
+        load_words(tabw[0], tab_words[0])
+        nc.sync.dma_start(idx2[:], offs2)
+        load_scales(tab2s, tab2_scales, 8)
+        load_words(tabw[1], tab_words[1])
+        load_w(0, 1)
+        load_words(tab2w[0], tab2_words[0])
+        nc.sync.dma_start(out=gain_t[:], in_=gain.rearrange("(b p t) -> p b t", b=2, t=PACK))
+        nc.sync.dma_start(p1[:], pos1)
+        nc.sync.dma_start(p2[:], pos2)
+        load_room(0)
+        load_w(1, 0)
+        nc.sync.dma_start(out=base_t[:], in_=base.rearrange("(b p t) -> p b t", b=2, t=PACK))
+        load_room(1)
+        load_w(1, 1)
+        load_room(2)
+        load_room(3)
+        for s in range(4, 8):
+            load_room(s)
+        load_words(tab2w[1], tab2_words[1])
+        with nc.allow_non_contiguous_dma(reason="one level a partition"):
+            nc.sync.dma_start(out=level_t[:], in_=level.rearrange("(m p) -> p m", p=P))
+
+        def slot(i, shape, dtype, name):
+            return keep.tile(shape, dtype, name=name, tag=f"slot{i}", align_bytes=64)
+
+        def round_w(copy, wb, b, a, t0, t1):
+            copy(
+                out=wb.rearrange("p (t m j) -> p m j t", t=PACK, j=PACK)[:, :, :, t0:t1],
+                in_=wraw[b][a][:].rearrange("p j (m t) -> p m j t", t=PACK)[:, :, :, t0:t1],
+            )
+
+        def quantise_w(wb, b, c0, c1):
+            nc.vector.quantize_mx(out=wq[b][:, c0:c1].bitcast(FP8X4), scales=ws[b][:, c0:c1], in_=wb)
+
+        def gather(dst, window, offsets):
+            nc.vector.tensor_copy(dst, window[:].indirect(offsets))
+
+        half = BANK // 16
+        wb = slot(0, [P, PACK * PASS], BF16, "wb00")
+        round_w(nc.scalar.copy, wb[:], 0, 0, 0, 4)
+        quantise_w(wb[:], 0, 0, PASS)
+        gather(vs[:], tabs, idx[:])
+        for n in range(2):
+            gather(vw[0][n][:], tabw[0], idx[:, n * half : (n + 1) * half])
+        gather(v2s[:], tab2s, idx2[:])
+        for n in range(2):
+            gather(vw[1][n][:], tabw[1], idx[:, n * half : (n + 1) * half])
+        wb = slot(1, [P, PACK * PASS], BF16, "wb01")
+        round_w(nc.vector.tensor_copy, wb[:], 0, 1, 0, 2)
+        round_w(nc.scalar.copy, wb[:], 0, 1, 2, 4)
+        quantise_w(wb[:, 0 : 2 * PASS], 0, PASS, PASS + 2 * P)
+        quantise_w(wb[:, 2 * PASS : 4 * PASS], 0, PASS + 2 * P, 2 * PASS)
+
+        def first_product(s):
+            b, t = divmod(s, PACK)
+            th = keep.tile([P, S], F32, name="th", tag=f"th{s % 2}", align_bytes=64)
+            for n in range(2):
+                acc = psum.tile([P, BANK], F32, name="acc")
+                for a in range(2):
+                    m = slice(a * PASS + t * P, a * PASS + (t + 1) * P)
+                    nc.tensor.matmul_mx(
+                        out=acc[:],
+                        lhsT=wq[b][:, m].bitcast(FP8X4),
+                        lhsT_scale=ws[b][:, m],
+                        rhs=vw[a][n][:].bitcast(FP8X4),
+                        rhs_scale=vs[4 * a : P, n * BANK : (n + 1) * BANK],
+                        start=(a == 0),
+                        stop=(a == 1),
+                    )
+                nc.scalar.activation(out=th[:, n * BANK : (n + 1) * BANK], in_=acc[:], func=ACT.Tanh)
+            return th
+
+        def times_gain(s, th):
+            b, t = divmod(s, PACK)
+            h = slot(s % 4, [P, S], F32, "h")
+            if s in GAIN_ON_VECTOR:
+                nc.vector.tensor_scalar(out=h[:], in0=th[:], scalar1=gain_t[:, b, t : t + 1], scalar2=None, op0=ALU.mult)
+            else:
+                nc.scalar.activation(out=h[:], in_=th[:], func=ACT.Copy, scale=gain_t[:, b, t : t + 1])
+            return h
+
+        def pick1(h, s, j0, width, g):
+            cols = slice(j0 // 16, (j0 + width) // 16)
+            nc.vector.tensor_tensor(g[:, s % PACK, :], h[:].indirect(p1[:, cols]), room_t[s][:, j0 : j0 + width], ALU.mult)
+
+        def pick2(h, s, j0, width, g):
+            cols = slice(j0 // 16, (j0 + width) // 16)
+            nc.vector.tensor_copy(g[:, s % PACK, :], h[:].indirect(p2[:, cols]))
+
+        def interleaved(xb):
+            return xb.rearrange("p (c i t) -> p c t i", i=4, t=PACK)
+
+        def by_rows(g):
+            return g.rearrange("p t (c i) -> p c t i", i=4)
+
+        def quantise_x(xb, width, name):
+            xq = held([P, width], U32, f"xq{name}")
+            xs = held([P, width], U8, f"xs{name}")
+            nc.vector.quantize_mx(out=xq[:].bitcast(FP8X4), scales=xs[:], in_=xb)
+            return xq, xs
+
+        g0 = [held([P, PACK, J], F32, f"g0{i}") for i in range(2)]
+
+        def picks0(h, s):
+            pick1(h, s, 0, J, g0[0])
+            pick2(h, s, 0, J, g0[1])
+            nc.vector.tensor_scalar(
+                out=g0[1][:, s, :], in0=g0[1][:, s, :], scalar1=base_t[:, 0, s : s + 1], scalar2=None, op0=ALU.max
+            )
+
+        th = first_product(0)
+        gather(v2w[0][:], tab2w[0], idx2[:])
+        h = times_gain(0, th)
+        th = first_product(1)
+        picks0(h, 0)
+        h = times_gain(1, th)
+        wb = slot(2, [P, 2, PACK * PASS], BF16, "wb1")
+        round_w(nc.scalar.copy, wb[:, 0, :], 1, 0, 0, 4)
+        picks0(h, 1)
+        th = first_product(2)
+        round_w(nc.scalar.copy, wb[:, 1, :], 1, 1, 0, 4)
+        quantise_w(wb[:].rearrange("p a c -> p (a c)"), 1, 0, 2 * PASS)
+        h = times_gain(2, th)
+        h3 = times_gain(3, first_product(3))
+        picks0(h, 2)
+        picks0(h3, 3)
+
+        hs = [times_gain(s, first_product(s)) for s in range(4, 8)]
+        xb0 = keep.tile([P, 2, PACK * J], BF16, name="xb0", tag="th1", align_bytes=64)
+        x0 = []
+        for i in range(2):
+            nc.scalar.copy(out=interleaved(xb0[:, i, :]), in_=by_rows(g0[i][:]))
+            x0.append(quantise_x(xb0[:, i, :], J, f"0{i}"))
+        gather(v2w[1][:], tab2w[1], idx2[:])
+        x1 = []
+        for c in range(2):
+            ga = held([P, PACK, CHUNK], F32, f"g1{c}")
+            gb = keep.tile([P, PACK, CHUNK], F32, name="gb", align_bytes=64)
+            for s in range(4, 8):
+                pick1(hs[s - 4], s, c * CHUNK, CHUNK, ga)
+                pick2(hs[s - 4], s, c * CHUNK, CHUNK, gb)
+            xa = held([P, PACK * CHUNK], BF16, f"xa{c}")
+            xb = held([P, PACK * CHUNK], BF16, f"xb{c}")
+            floor = base_t[:, 1, :].unsqueeze(1).unsqueeze(3).to_broadcast([P, CHUNK // 4, PACK, 4])
+            nc.vector.tensor_tensor(interleaved(xb[:]), by_rows(gb[:]), floor, ALU.max)
+            nc.scalar.copy(out=interleaved(xa[:]), in_=by_rows(ga[:]))
+            x1.append([quantise_x(xa[:], CHUNK, f"1{c}0"), quantise_x(xb[:], CHUNK, f"1{c}1")])
+
+        for c in range(2):
+            cols = slice(c * CHUNK, (c + 1) * CHUNK)
+            for mp in range(2):
+                e = [psum.tile([P, 2, CHUNK], F32, name="acc") for i in range(2)]
+                for b in range(2):
+                    for i in (1, 0):
+                        for u in range(2):
+                            m = slice((2 * mp + u) * P, (2 * mp + u + 1) * P)
+                            xq, xs = x0[i] if b == 0 else x1[c][i]
+                            xcols = cols if b == 0 else slice(0, CHUNK)
+                            nc.tensor.matmul_mx(
+                                out=e[i][:, u, :],
+                                lhsT=v2w[b][:, m].bitcast(FP8X4),
+                                lhsT_scale=v2s[8 + 4 * b : P, m],
+                                rhs=xq[:, xcols].bitcast(FP8X4),
+                                rhs_scale=xs[:, xcols],
+                                start=(b == 0 and u == 0),
+                                stop=(b == 1 and u == 1),
+                            )
+                e2 = ring.tile([P, 2, CHUNK], F32, name="e2")
+                nc.scalar.copy(out=e2[:], in_=e[1][:])
+                prod = ring.tile([P, 2, CHUNK], F32, name="prod")
+                nc.vector.tensor_tensor(prod[:], e[0][:], e2[:], ALU.mult)
+                res = ring.tile([P, 2, CHUNK], F32, name="res")
+                for u in range(2):
+                    mt = 2 * mp + u
+                    nc.vector.scalar_tensor_tensor(
+                        out=res[:, u, :],
+                        in0=e[0][:, u, :],
+                        scalar=level_t[:, mt : mt + 1],
+                        in1=prod[:, u, :],
+                        op0=ALU.max,
+                        op1=ALU.add,
+                    )
+                rows = out[2 * mp * P : (2 * mp + 2) * P, cols]
+                nc.sync.dma_start(out=rows.rearrange("(u p) j -> p u j", p=P), in_=res[:])

@@ -70,13 +70,15 @@ def tile_list_showroom_lamp_scores_kernel(
 
         def load_scales(dst, scales, first):
             nc.vector.memset(dst[:].bitcast(I32), 0)
-            for q in range(4):
-                nc.sync.dma_start(
+            for q in (0, 2, 1, 3):
+                nc.gpsimd.dma_start(
                     out=dst[32 * q + first : 32 * q + first + 8, :].bitcast(I32),
                     in_=scales[:, 4 * q : 4 * q + 4, :].bitcast(I32),
                 )
 
         load_w(0, 0)
+        nc.scalar.dma_start(out=gain_t[:], in_=gain.rearrange("(b p t) -> p b t", b=2, t=PACK))
+        nc.scalar.dma_start(out=base_t[:], in_=base.rearrange("(b p t) -> p b t", b=2, t=PACK))
         load_scales(tabs, tab_scales, 0)
         nc.sync.dma_start(idx[:], offs)
         load_words(tabw[0], tab_words[0])
@@ -85,12 +87,10 @@ def tile_list_showroom_lamp_scores_kernel(
         load_words(tabw[1], tab_words[1])
         load_w(0, 1)
         load_words(tab2w[0], tab2_words[0])
-        nc.sync.dma_start(out=gain_t[:], in_=gain.rearrange("(b p t) -> p b t", b=2, t=PACK))
         nc.sync.dma_start(p1[:], pos1)
         nc.sync.dma_start(p2[:], pos2)
         load_room(0)
         load_w(1, 0)
-        nc.sync.dma_start(out=base_t[:], in_=base.rearrange("(b p t) -> p b t", b=2, t=PACK))
         load_room(1)
         load_w(1, 1)
         load_room(2)
@@ -104,10 +104,10 @@ def tile_list_showroom_lamp_scores_kernel(
         def slot(i, shape, dtype, name):
             return keep.tile(shape, dtype, name=name, tag=f"slot{i}", align_bytes=64)
 
-        def round_w(copy, wb, b, a, t0, t1):
+        def round_w(copy, wb, b, a, u0, u1):
             copy(
-                out=wb.rearrange("p (t m j) -> p m j t", t=PACK, j=PACK)[:, :, :, t0:t1],
-                in_=wraw[b][a][:].rearrange("p j (m t) -> p m j t", t=PACK)[:, :, :, t0:t1],
+                out=wb.rearrange("p (u t m j) -> p u m j t", u=2, t=2, j=PACK)[:, u0:u1],
+                in_=wraw[b][a][:].rearrange("p j (m u t) -> p u m j t", u=2, t=2)[:, u0:u1],
             )
 
         def quantise_w(wb, b, c0, c1):
@@ -118,7 +118,7 @@ def tile_list_showroom_lamp_scores_kernel(
 
         half = BANK // 16
         wb = slot(0, [P, PACK * PASS], BF16, "wb00")
-        round_w(nc.scalar.copy, wb[:], 0, 0, 0, 4)
+        round_w(nc.scalar.copy, wb[:], 0, 0, 0, 2)
         quantise_w(wb[:], 0, 0, PASS)
         gather(vs[:], tabs, idx[:])
         for n in range(2):
@@ -127,8 +127,8 @@ def tile_list_showroom_lamp_scores_kernel(
         for n in range(2):
             gather(vw[1][n][:], tabw[1], idx[:, n * half : (n + 1) * half])
         wb = slot(1, [P, PACK * PASS], BF16, "wb01")
-        round_w(nc.vector.tensor_copy, wb[:], 0, 1, 0, 2)
-        round_w(nc.scalar.copy, wb[:], 0, 1, 2, 4)
+        round_w(nc.vector.tensor_copy, wb[:], 0, 1, 0, 1)
+        round_w(nc.scalar.copy, wb[:], 0, 1, 1, 2)
         quantise_w(wb[:, 0 : 2 * PASS], 0, PASS, PASS + 2 * P)
         quantise_w(wb[:, 2 * PASS : 4 * PASS], 0, PASS + 2 * P, 2 * PASS)
 
@@ -166,7 +166,11 @@ def tile_list_showroom_lamp_scores_kernel(
 
         def pick2(h, s, j0, width, g):
             cols = slice(j0 // 16, (j0 + width) // 16)
-            nc.vector.tensor_copy(g[:, s % PACK, :], h[:].indirect(p2[:, cols]))
+            b, t = divmod(s, PACK)
+            nc.vector.tensor_copy(g[:, t, :], h[:].indirect(p2[:, cols]))
+            nc.vector.tensor_scalar(
+                out=g[:, t, :], in0=g[:, t, :], scalar1=base_t[:, b, t : t + 1], scalar2=None, op0=ALU.max
+            )
 
         def interleaved(xb):
             return xb.rearrange("p (c i t) -> p c t i", i=4, t=PACK)
@@ -185,9 +189,6 @@ def tile_list_showroom_lamp_scores_kernel(
         def picks0(h, s):
             pick1(h, s, 0, J, g0[0])
             pick2(h, s, 0, J, g0[1])
-            nc.vector.tensor_scalar(
-                out=g0[1][:, s, :], in0=g0[1][:, s, :], scalar1=base_t[:, 0, s : s + 1], scalar2=None, op0=ALU.max
-            )
 
         th = first_product(0)
         gather(v2w[0][:], tab2w[0], idx2[:])
@@ -196,10 +197,10 @@ def tile_list_showroom_lamp_scores_kernel(
         picks0(h, 0)
         h = times_gain(1, th)
         wb = slot(2, [P, 2, PACK * PASS], BF16, "wb1")
-        round_w(nc.scalar.copy, wb[:, 0, :], 1, 0, 0, 4)
+        round_w(nc.scalar.copy, wb[:, 0, :], 1, 0, 0, 2)
         picks0(h, 1)
         th = first_product(2)
-        round_w(nc.scalar.copy, wb[:, 1, :], 1, 1, 0, 4)
+        round_w(nc.scalar.copy, wb[:, 1, :], 1, 1, 0, 2)
         quantise_w(wb[:].rearrange("p a c -> p (a c)"), 1, 0, 2 * PASS)
         h = times_gain(2, th)
         h3 = times_gain(3, first_product(3))
@@ -222,8 +223,7 @@ def tile_list_showroom_lamp_scores_kernel(
                 pick2(hs[s - 4], s, c * CHUNK, CHUNK, gb)
             xa = held([P, PACK * CHUNK], BF16, f"xa{c}")
             xb = held([P, PACK * CHUNK], BF16, f"xb{c}")
-            floor = base_t[:, 1, :].unsqueeze(1).unsqueeze(3).to_broadcast([P, CHUNK // 4, PACK, 4])
-            nc.vector.tensor_tensor(interleaved(xb[:]), by_rows(gb[:]), floor, ALU.max)
+            nc.vector.tensor_copy(out=interleaved(xb[:]), in_=by_rows(gb[:]))
             nc.scalar.copy(out=interleaved(xa[:]), in_=by_rows(ga[:]))
             x1.append([quantise_x(xa[:], CHUNK, f"1{c}0"), quantise_x(xb[:], CHUNK, f"1{c}1")])
 
@@ -261,5 +261,4 @@ def tile_list_showroom_lamp_scores_kernel(
                         op0=ALU.max,
                         op1=ALU.add,
                     )
-                rows = out[2 * mp * P : (2 * mp + 2) * P, cols]
-                nc.sync.dma_start(out=rows.rearrange("(u p) j -> p u j", p=P), in_=res[:])
+                    nc.sync.dma_start(out=out[mt * P : (mt + 1) * P, cols], in_=res[:, u, :])

@@ -46,7 +46,7 @@ def tile_list_showroom_lamp_scores_kernel(
         tab2s = held([P, T2], U8, "tab2s")
         vw = [[held([P, BANK], U32, f"vw{a}{n}") for n in range(2)] for a in range(2)]
         vs = held([P, S], U8, "vs")
-        v2w = [held([P, S2], U32, f"v2w{b}") for b in range(2)]
+        v2g = held([P, S2], U8, "v2g")
         v2s = held([P, S2], U8, "v2s")
         wraw = [[held([P, PACK, PASS], F32, f"wraw{b}{a}") for a in range(2)] for b in range(2)]
         wq = [held([P, 2 * PASS], U32, f"wq{b}") for b in range(2)]
@@ -68,36 +68,36 @@ def tile_list_showroom_lamp_scores_kernel(
             rows = room[b * PASS : (b + 1) * PASS, :].rearrange("(p t) j -> p t j", t=PACK)
             nc.sync.dma_start(out=room_t[s][:], in_=rows[:, t, :])
 
-        def load_scales(dst, scales, first):
-            nc.vector.memset(dst[:].bitcast(I32), 0)
-            for q in (0, 2, 1, 3):
-                nc.gpsimd.dma_start(
-                    out=dst[32 * q + first : 32 * q + first + 8, :].bitcast(I32),
-                    in_=scales[:, 4 * q : 4 * q + 4, :].bitcast(I32),
-                )
-
+        nc.vector.memset(tab2s[:].bitcast(I32), 0)
+        nc.vector.memset(tabs[:].bitcast(I32), 0)
+        nc.vector.memset(v2s[:].bitcast(I32), 0)
         load_w(0, 0)
-        nc.scalar.dma_start(out=gain_t[:], in_=gain.rearrange("(b p t) -> p b t", b=2, t=PACK))
-        nc.scalar.dma_start(out=base_t[:], in_=base.rearrange("(b p t) -> p b t", b=2, t=PACK))
-        load_scales(tabs, tab_scales, 0)
+        nc.sync.dma_start(idx2[:], offs2)
+        nc.sync.dma_start(
+            out=tab2s[0:P:4, :].bitcast(I32), in_=tab2_scales.rearrange("b q t -> (b q) t").bitcast(I32)
+        )
         nc.sync.dma_start(idx[:], offs)
         load_words(tabw[0], tab_words[0])
-        nc.sync.dma_start(idx2[:], offs2)
-        load_scales(tab2s, tab2_scales, 8)
+        for q in (0, 2, 1, 3):
+            nc.sync.dma_start(
+                out=tabs[32 * q : 32 * q + 8, :].bitcast(I32), in_=tab_scales[:, 4 * q : 4 * q + 4, :].bitcast(I32)
+            )
         load_words(tabw[1], tab_words[1])
         load_w(0, 1)
-        load_words(tab2w[0], tab2_words[0])
+        nc.sync.dma_start(out=gain_t[:], in_=gain.rearrange("(b p t) -> p b t", b=2, t=PACK))
         nc.sync.dma_start(p1[:], pos1)
         nc.sync.dma_start(p2[:], pos2)
         load_room(0)
         load_w(1, 0)
+        nc.sync.dma_start(out=base_t[:], in_=base.rearrange("(b p t) -> p b t", b=2, t=PACK))
         load_room(1)
         load_w(1, 1)
         load_room(2)
         load_room(3)
+        load_words(tab2w[0], tab2_words[0])
+        load_words(tab2w[1], tab2_words[1])
         for s in range(4, 8):
             load_room(s)
-        load_words(tab2w[1], tab2_words[1])
         with nc.allow_non_contiguous_dma(reason="one level a partition"):
             nc.sync.dma_start(out=level_t[:], in_=level.rearrange("(m p) -> p m", p=P))
 
@@ -120,10 +120,17 @@ def tile_list_showroom_lamp_scores_kernel(
         wb = slot(0, [P, PACK * PASS], BF16, "wb00")
         round_w(nc.scalar.copy, wb[:], 0, 0, 0, 2)
         quantise_w(wb[:], 0, 0, PASS)
-        gather(vs[:], tabs, idx[:])
+        gather(v2g[:], tab2s, idx2[:])
+        for b in range(2):
+            for q in range(4):
+                row = 4 * (16 * b + 4 * q)
+                nc.sync.dma_start(
+                    out=v2s[32 * q + 4 * b : 32 * q + 4 * b + 4, :].bitcast(I32),
+                    in_=v2g[row : row + 16 : 4, :].bitcast(I32),
+                )
         for n in range(2):
             gather(vw[0][n][:], tabw[0], idx[:, n * half : (n + 1) * half])
-        gather(v2s[:], tab2s, idx2[:])
+        gather(vs[:], tabs, idx[:])
         for n in range(2):
             gather(vw[1][n][:], tabw[1], idx[:, n * half : (n + 1) * half])
         wb = slot(1, [P, PACK * PASS], BF16, "wb01")
@@ -155,7 +162,12 @@ def tile_list_showroom_lamp_scores_kernel(
             b, t = divmod(s, PACK)
             h = slot(s % 4, [P, S], F32, "h")
             if s in GAIN_ON_VECTOR:
-                nc.vector.tensor_scalar(out=h[:], in0=th[:], scalar1=gain_t[:, b, t : t + 1], scalar2=None, op0=ALU.mult)
+                width = BANK if s == 0 else S
+                for n0 in range(0, S, width):
+                    cols = slice(n0, n0 + width)
+                    nc.vector.tensor_scalar(
+                        out=h[:, cols], in0=th[:, cols], scalar1=gain_t[:, b, t : t + 1], scalar2=None, op0=ALU.mult
+                    )
             else:
                 nc.scalar.activation(out=h[:], in_=th[:], func=ACT.Copy, scale=gain_t[:, b, t : t + 1])
             return h
@@ -190,22 +202,28 @@ def tile_list_showroom_lamp_scores_kernel(
             pick1(h, s, 0, J, g0[0])
             pick2(h, s, 0, J, g0[1])
 
-        th = first_product(0)
-        gather(v2w[0][:], tab2w[0], idx2[:])
-        h = times_gain(0, th)
+        def second_half_of_w(a):
+            wb = slot(1 + a, [P, PACK * PASS], BF16, "wb1")
+            round_w(nc.scalar.copy, wb[:], 1, a, 0, 2)
+            quantise_w(wb[:], 1, a * PASS, (a + 1) * PASS)
+
+        def lamps(b):
+            v2w = keep.tile([P, S2], U32, name="v2w", tag=f"room{2 + b}", align_bytes=64)
+            gather(v2w[:], tab2w[b], idx2[:])
+            return v2w
+
+        h = times_gain(0, first_product(0))
         th = first_product(1)
         picks0(h, 0)
-        h = times_gain(1, th)
-        wb = slot(2, [P, 2, PACK * PASS], BF16, "wb1")
-        round_w(nc.scalar.copy, wb[:, 0, :], 1, 0, 0, 2)
-        picks0(h, 1)
+        second_half_of_w(0)
+        picks0(times_gain(1, th), 1)
         th = first_product(2)
-        round_w(nc.scalar.copy, wb[:, 1, :], 1, 1, 0, 2)
-        quantise_w(wb[:].rearrange("p a c -> p (a c)"), 1, 0, 2 * PASS)
+        second_half_of_w(1)
         h = times_gain(2, th)
         h3 = times_gain(3, first_product(3))
         picks0(h, 2)
         picks0(h3, 3)
+        v2w = [lamps(b) for b in range(2)]
 
         hs = [times_gain(s, first_product(s)) for s in range(4, 8)]
         xb0 = keep.tile([P, 2, PACK * J], BF16, name="xb0", tag="th1", align_bytes=64)
@@ -213,7 +231,6 @@ def tile_list_showroom_lamp_scores_kernel(
         for i in range(2):
             nc.scalar.copy(out=interleaved(xb0[:, i, :]), in_=by_rows(g0[i][:]))
             x0.append(quantise_x(xb0[:, i, :], J, f"0{i}"))
-        gather(v2w[1][:], tab2w[1], idx2[:])
         x1 = []
         for c in range(2):
             ga = held([P, PACK, CHUNK], F32, f"g1{c}")
@@ -223,7 +240,8 @@ def tile_list_showroom_lamp_scores_kernel(
                 pick2(hs[s - 4], s, c * CHUNK, CHUNK, gb)
             xa = held([P, PACK * CHUNK], BF16, f"xa{c}")
             xb = held([P, PACK * CHUNK], BF16, f"xb{c}")
-            nc.vector.tensor_copy(out=interleaved(xb[:]), in_=by_rows(gb[:]))
+            copy = nc.scalar.copy if c == 0 else nc.vector.tensor_copy
+            copy(out=interleaved(xb[:]), in_=by_rows(gb[:]))
             nc.scalar.copy(out=interleaved(xa[:]), in_=by_rows(ga[:]))
             x1.append([quantise_x(xa[:], CHUNK, f"1{c}0"), quantise_x(xb[:], CHUNK, f"1{c}1")])
 
@@ -240,7 +258,7 @@ def tile_list_showroom_lamp_scores_kernel(
                             nc.tensor.matmul_mx(
                                 out=e[i][:, u, :],
                                 lhsT=v2w[b][:, m].bitcast(FP8X4),
-                                lhsT_scale=v2s[8 + 4 * b : P, m],
+                                lhsT_scale=v2s[4 * b : P, m],
                                 rhs=xq[:, xcols].bitcast(FP8X4),
                                 rhs_scale=xs[:, xcols],
                                 start=(b == 0 and u == 0),

@@ -20,7 +20,7 @@ PACK = 4
 PASS = P * PACK
 BANK = 512
 CHUNK = 256
-GAIN_ON_VECTOR = (0, 1, 2)
+GAIN_ON_VECTOR = (0,)
 
 
 def tile_list_showroom_lamp_scores_kernel(
@@ -51,7 +51,9 @@ def tile_list_showroom_lamp_scores_kernel(
         wraw = [[held([P, PACK, PASS], F32, f"wraw{b}{a}") for a in range(2)] for b in range(2)]
         wq = [held([P, 2 * PASS], U32, f"wq{b}") for b in range(2)]
         ws = [held([P, 2 * PASS], U8, f"ws{b}") for b in range(2)]
-        room_t = [held([P, J], F32, f"room{s}") for s in range(8)]
+        room_groups = ((0, 1), (1, 2), (2, 4), (4, 8))
+        room_tiles = [held([P, s1 - s0, J], F32, f"room{s0}") for s0, s1 in room_groups]
+        room_t = [tile[:, s - s0, :] for tile, (s0, s1) in zip(room_tiles, room_groups) for s in range(s0, s1)]
         gain_t = held([P, 2, PACK], F32, "gain_t")
         base_t = held([P, 2, PACK], F32, "base_t")
         level_t = held([P, 4], F32, "level_t")
@@ -63,10 +65,11 @@ def tile_list_showroom_lamp_scores_kernel(
         def load_words(dst, words):
             nc.sync.dma_start(out=dst[:].bitcast(I32), in_=words.rearrange("p t i -> p (t i)").bitcast(I32))
 
-        def load_room(s):
-            b, t = divmod(s, PACK)
+        def load_room(i):
+            s0, s1 = room_groups[i]
+            b, t = divmod(s0, PACK)
             rows = room[b * PASS : (b + 1) * PASS, :].rearrange("(p t) j -> p t j", t=PACK)
-            nc.sync.dma_start(out=room_t[s][:], in_=rows[:, t, :])
+            nc.sync.dma_start(out=room_tiles[i][:], in_=rows[:, t : t + s1 - s0, :])
 
         nc.vector.memset(tab2s[:].bitcast(I32), 0)
         nc.vector.memset(tabs[:].bitcast(I32), 0)
@@ -93,11 +96,9 @@ def tile_list_showroom_lamp_scores_kernel(
         load_room(1)
         load_w(1, 1)
         load_room(2)
-        load_room(3)
         load_words(tab2w[0], tab2_words[0])
         load_words(tab2w[1], tab2_words[1])
-        for s in range(4, 8):
-            load_room(s)
+        load_room(3)
         with nc.allow_non_contiguous_dma(reason="one level a partition"):
             nc.sync.dma_start(out=level_t[:], in_=level.rearrange("(m p) -> p m", p=P))
 
@@ -117,7 +118,7 @@ def tile_list_showroom_lamp_scores_kernel(
             nc.vector.tensor_copy(dst, window[:].indirect(offsets))
 
         half = BANK // 16
-        wb = slot(0, [P, PACK * PASS], BF16, "wb00")
+        wb = held([P, PACK * PASS], BF16, "wb")
         round_w(nc.scalar.copy, wb[:], 0, 0, 0, 2)
         quantise_w(wb[:], 0, 0, PASS)
         gather(v2g[:], tab2s, idx2[:])
@@ -133,7 +134,7 @@ def tile_list_showroom_lamp_scores_kernel(
         gather(vs[:], tabs, idx[:])
         for n in range(2):
             gather(vw[1][n][:], tabw[1], idx[:, n * half : (n + 1) * half])
-        wb = slot(1, [P, PACK * PASS], BF16, "wb01")
+        wb = held([P, PACK * PASS], BF16, "wb")
         round_w(nc.vector.tensor_copy, wb[:], 0, 1, 0, 1)
         round_w(nc.scalar.copy, wb[:], 0, 1, 1, 2)
         quantise_w(wb[:, 0 : 2 * PASS], 0, PASS, PASS + 2 * P)
@@ -178,8 +179,10 @@ def tile_list_showroom_lamp_scores_kernel(
 
         def pick2(h, s, j0, width, g):
             cols = slice(j0 // 16, (j0 + width) // 16)
+            nc.vector.tensor_copy(g[:, s % PACK, :], h[:].indirect(p2[:, cols]))
+
+        def floor(s, g):
             b, t = divmod(s, PACK)
-            nc.vector.tensor_copy(g[:, t, :], h[:].indirect(p2[:, cols]))
             nc.vector.tensor_scalar(
                 out=g[:, t, :], in0=g[:, t, :], scalar1=base_t[:, b, t : t + 1], scalar2=None, op0=ALU.max
             )
@@ -199,18 +202,14 @@ def tile_list_showroom_lamp_scores_kernel(
         g0 = [held([P, PACK, J], F32, f"g0{i}") for i in range(2)]
 
         def picks0(h, s):
-            pick1(h, s, 0, J, g0[0])
             pick2(h, s, 0, J, g0[1])
+            pick1(h, s, 0, J, g0[0])
+            floor(s, g0[1])
 
         def second_half_of_w(a):
-            wb = slot(1 + a, [P, PACK * PASS], BF16, "wb1")
+            wb = held([P, PACK * PASS], BF16, "wb")
             round_w(nc.scalar.copy, wb[:], 1, a, 0, 2)
             quantise_w(wb[:], 1, a * PASS, (a + 1) * PASS)
-
-        def lamps(b):
-            v2w = keep.tile([P, S2], U32, name="v2w", tag=f"room{2 + b}", align_bytes=64)
-            gather(v2w[:], tab2w[b], idx2[:])
-            return v2w
 
         h = times_gain(0, first_product(0))
         th = first_product(1)
@@ -223,7 +222,9 @@ def tile_list_showroom_lamp_scores_kernel(
         h3 = times_gain(3, first_product(3))
         picks0(h, 2)
         picks0(h3, 3)
-        v2w = [lamps(b) for b in range(2)]
+        v2w = [held([P, S2], U32, "v2w0"), keep.tile([P, S2], U32, name="v2w1", tag="wb", align_bytes=64)]
+        for b in range(2):
+            gather(v2w[b][:], tab2w[b], idx2[:])
 
         hs = [times_gain(s, first_product(s)) for s in range(4, 8)]
         xb0 = keep.tile([P, 2, PACK * J], BF16, name="xb0", tag="th1", align_bytes=64)
@@ -232,17 +233,20 @@ def tile_list_showroom_lamp_scores_kernel(
             nc.scalar.copy(out=interleaved(xb0[:, i, :]), in_=by_rows(g0[i][:]))
             x0.append(quantise_x(xb0[:, i, :], J, f"0{i}"))
         x1 = []
+        ga = held([P, PACK, J], F32, "ga")
         for c in range(2):
-            ga = held([P, PACK, CHUNK], F32, f"g1{c}")
-            gb = keep.tile([P, PACK, CHUNK], F32, name="gb", align_bytes=64)
+            gb = keep.tile([P, PACK, CHUNK], F32, name="gb", tag=("gb", "th1")[c], align_bytes=64)
             for s in range(4, 8):
-                pick1(hs[s - 4], s, c * CHUNK, CHUNK, ga)
                 pick2(hs[s - 4], s, c * CHUNK, CHUNK, gb)
+                if c == 0:
+                    pick1(hs[s - 4], s, 0, J, ga)
+            for s in range(4, 8):
+                floor(s, gb)
             xa = held([P, PACK * CHUNK], BF16, f"xa{c}")
             xb = held([P, PACK * CHUNK], BF16, f"xb{c}")
             copy = nc.scalar.copy if c == 0 else nc.vector.tensor_copy
             copy(out=interleaved(xb[:]), in_=by_rows(gb[:]))
-            nc.scalar.copy(out=interleaved(xa[:]), in_=by_rows(ga[:]))
+            nc.scalar.copy(out=interleaved(xa[:]), in_=by_rows(ga[:, :, c * CHUNK : (c + 1) * CHUNK]))
             x1.append([quantise_x(xa[:], CHUNK, f"1{c}0"), quantise_x(xb[:], CHUNK, f"1{c}1")])
 
         for c in range(2):
@@ -267,7 +271,8 @@ def tile_list_showroom_lamp_scores_kernel(
                 e2 = ring.tile([P, 2, CHUNK], F32, name="e2")
                 nc.scalar.copy(out=e2[:], in_=e[1][:])
                 prod = ring.tile([P, 2, CHUNK], F32, name="prod")
-                nc.vector.tensor_tensor(prod[:], e[0][:], e2[:], ALU.mult)
+                for u in range(2):
+                    nc.vector.tensor_tensor(prod[:, u, :], e[0][:, u, :], e2[:, u, :], ALU.mult)
                 res = ring.tile([P, 2, CHUNK], F32, name="res")
                 for u in range(2):
                     mt = 2 * mp + u

@@ -21,6 +21,7 @@ PASS = P * PACK
 BANK = 512
 CHUNK = 256
 GAIN_ON_VECTOR = (0,)
+F32_MAX = 3.4028234663852886e38
 
 
 def tile_list_showroom_lamp_scores_kernel(
@@ -181,6 +182,17 @@ def tile_list_showroom_lamp_scores_kernel(
             cols = slice(j0 // 16, (j0 + width) // 16)
             nc.vector.tensor_copy(g[:, s % PACK, :], h[:].indirect(p2[:, cols]))
 
+        def floor_aside(s, g):
+            b, t = divmod(s, PACK)
+            nc.gpsimd.tensor_scalar(
+                out=g[:, t, :],
+                in0=g[:, t, :],
+                scalar1=F32_MAX,
+                scalar2=base_t[:, b, t : t + 1],
+                op0=ALU.min,
+                op1=ALU.max,
+            )
+
         def floor(s, g):
             b, t = divmod(s, PACK)
             nc.vector.tensor_scalar(
@@ -204,7 +216,7 @@ def tile_list_showroom_lamp_scores_kernel(
         def picks0(h, s):
             pick2(h, s, 0, J, g0[1])
             pick1(h, s, 0, J, g0[0])
-            floor(s, g0[1])
+            floor_aside(s, g0[1])
 
         def second_half_of_w(a):
             wb = held([P, PACK * PASS], BF16, "wb")
@@ -241,7 +253,7 @@ def tile_list_showroom_lamp_scores_kernel(
                 if c == 0:
                     pick1(hs[s - 4], s, 0, J, ga)
             for s in range(4, 8):
-                floor(s, gb)
+                (floor_aside, floor)[c](s, gb)
             xa = held([P, PACK * CHUNK], BF16, f"xa{c}")
             xb = held([P, PACK * CHUNK], BF16, f"xb{c}")
             copy = nc.scalar.copy if c == 0 else nc.vector.tensor_copy

from contextlib import ExitStack

import concourse.mybir as mybir

K, T, S, H, T2, S2, J = 1024, 4096, 1024, 1024, 2048, 512, 512
FLOPS = 2 * K * H * S + 2 * 2 * H * S2 * J

F32 = mybir.dt.float32
BF16 = mybir.dt.bfloat16
I32 = mybir.dt.int32
U32 = mybir.dt.uint32
U16 = mybir.dt.uint16
U8 = mybir.dt.uint8
FP8X4 = mybir.dt.float8_e4m3fn_x4
ACT = mybir.ActivationFunctionType
ALU = mybir.AluOpType

P = 128
PACK = 4
PASS = P * PACK
BANK = 512
CHUNK = 256
GAIN_ON_VECTOR = (0,)
F32_MAX = 3.4028234663852886e38


def tile_list_showroom_lamp_scores_kernel(
    tc, tab_words, tab_scales, offs, tab2_words, tab2_scales, offs2, pos1, pos2, w1, gain, room, base, level, out
):
    nc = tc.nc
    with ExitStack() as ctx:
        keep = ctx.enter_context(tc.tile_pool(name="keep", bufs=1))
        ring = ctx.enter_context(tc.tile_pool(name="ring", bufs=2))
        psum = ctx.enter_context(tc.psum_pool(name="psum", bufs=8))

        def held(shape, dtype, name):
            return keep.tile(shape, dtype, name=name, align_bytes=64)

        idx = keep.tile([P, S // 16], U16, name="idx")
        idx2 = keep.tile([P, S2 // 16], U16, name="idx2")
        p1 = keep.tile([P, J // 16], U16, name="p1")
        p2 = keep.tile([P, J // 16], U16, name="p2")

        tabw = [held([P, T], U32, f"tabw{a}") for a in range(2)]
        tabs = held([P, T], U8, "tabs")
        tab2w = [held([P, T2], U32, f"tab2w{b}") for b in range(2)]
        tab2s = held([P, T2], U8, "tab2s")
        vw = [[held([P, BANK], U32, f"vw{a}{n}") for n in range(2)] for a in range(2)]
        vs = held([P, S], U8, "vs")
        v2g = held([P, S2], U8, "v2g")
        v2s = held([P, S2], U8, "v2s")
        wraw = [[held([P, PACK, PASS], F32, f"wraw{b}{a}") for a in range(2)] for b in range(2)]
        wq = [held([P, 2 * PASS], U32, f"wq{b}") for b in range(2)]
        ws = [held([P, 2 * PASS], U8, f"ws{b}") for b in range(2)]
        room_groups = ((0, 1), (1, 2), (2, 4), (4, 8))
        room_tiles = [held([P, s1 - s0, J], F32, f"room{s0}") for s0, s1 in room_groups]
        room_t = [tile[:, s - s0, :] for tile, (s0, s1) in zip(room_tiles, room_groups) for s in range(s0, s1)]
        gain_t = held([P, 2, PACK], F32, "gain_t")
        base_t = held([P, 2, PACK], F32, "base_t")
        level_t = held([P, 4], F32, "level_t")

        def load_w(b, a):
            rows = w1[a * PASS : (a + 1) * PASS, b * PASS : (b + 1) * PASS]
            nc.sync.dma_start(out=wraw[b][a][:], in_=rows.rearrange("(p j) c -> p j c", j=PACK))

        def load_words(dst, words):
            nc.sync.dma_start(out=dst[:].bitcast(I32), in_=words.rearrange("p t i -> p (t i)").bitcast(I32))

        def load_room(i):
            s0, s1 = room_groups[i]
            b, t = divmod(s0, PACK)
            rows = room[b * PASS : (b + 1) * PASS, :].rearrange("(p t) j -> p t j", t=PACK)
            nc.sync.dma_start(out=room_tiles[i][:], in_=rows[:, t : t + s1 - s0, :])

        nc.vector.memset(tab2s[:].bitcast(I32), 0)
        nc.vector.memset(tabs[:].bitcast(I32), 0)
        nc.vector.memset(v2s[:].bitcast(I32), 0)
        load_w(0, 0)
        nc.sync.dma_start(idx2[:], offs2)
        nc.sync.dma_start(
            out=tab2s[0:P:4, :].bitcast(I32), in_=tab2_scales.rearrange("b q t -> (b q) t").bitcast(I32)
        )
        nc.sync.dma_start(idx[:], offs)
        load_words(tabw[0], tab_words[0])
        for q in (0, 2, 1, 3):
            nc.sync.dma_start(
                out=tabs[32 * q : 32 * q + 8, :].bitcast(I32), in_=tab_scales[:, 4 * q : 4 * q + 4, :].bitcast(I32)
            )
        load_words(tabw[1], tab_words[1])
        load_w(0, 1)
        nc.sync.dma_start(out=gain_t[:], in_=gain.rearrange("(b p t) -> p b t", b=2, t=PACK))
        nc.sync.dma_start(p1[:], pos1)
        nc.sync.dma_start(p2[:], pos2)
        load_room(0)
        load_w(1, 0)
        nc.sync.dma_start(out=base_t[:], in_=base.rearrange("(b p t) -> p b t", b=2, t=PACK))
        load_room(1)
        load_w(1, 1)
        load_room(2)
        load_words(tab2w[0], tab2_words[0])
        load_words(tab2w[1], tab2_words[1])
        load_room(3)
        with nc.allow_non_contiguous_dma(reason="one level a partition"):
            nc.sync.dma_start(out=level_t[:], in_=level.rearrange("(m p) -> p m", p=P))

        def slot(i, shape, dtype, name):
            return keep.tile(shape, dtype, name=name, tag=f"slot{i}", align_bytes=64)

        def round_w(copy, wb, b, a, u0, u1):
            copy(
                out=wb.rearrange("p (u t m j) -> p u m j t", u=2, t=2, j=PACK)[:, u0:u1],
                in_=wraw[b][a][:].rearrange("p j (m u t) -> p u m j t", u=2, t=2)[:, u0:u1],
            )

        def quantise_w(wb, b, c0, c1):
            nc.vector.quantize_mx(out=wq[b][:, c0:c1].bitcast(FP8X4), scales=ws[b][:, c0:c1], in_=wb)

        def gather(dst, window, offsets):
            nc.vector.tensor_copy(dst, window[:].indirect(offsets))

        half = BANK // 16
        wb = held([P, PACK * PASS], BF16, "wb")
        round_w(nc.scalar.copy, wb[:], 0, 0, 0, 2)
        quantise_w(wb[:], 0, 0, PASS)
        gather(v2g[:], tab2s, idx2[:])
        for b in range(2):
            for q in range(4):
                row = 4 * (16 * b + 4 * q)
                nc.sync.dma_start(
                    out=v2s[32 * q + 4 * b : 32 * q + 4 * b + 4, :].bitcast(I32),
                    in_=v2g[row : row + 16 : 4, :].bitcast(I32),
                )
        for n in range(2):
            gather(vw[0][n][:], tabw[0], idx[:, n * half : (n + 1) * half])
        gather(vs[:], tabs, idx[:])
        for n in range(2):
            gather(vw[1][n][:], tabw[1], idx[:, n * half : (n + 1) * half])
        wb = held([P, PACK * PASS], BF16, "wb")
        round_w(nc.vector.tensor_copy, wb[:], 0, 1, 0, 1)
        round_w(nc.scalar.copy, wb[:], 0, 1, 1, 2)
        quantise_w(wb[:, 0 : 2 * PASS], 0, PASS, PASS + 2 * P)
        quantise_w(wb[:, 2 * PASS : 4 * PASS], 0, PASS + 2 * P, 2 * PASS)

        def first_product(s):
            b, t = divmod(s, PACK)
            th = keep.tile([P, S], F32, name="th", tag=f"th{s % 2}", align_bytes=64)
            for n in range(2):
                acc = psum.tile([P, BANK], F32, name="acc")
                for a in range(2):
                    m = slice(a * PASS + t * P, a * PASS + (t + 1) * P)
                    nc.tensor.matmul_mx(
                        out=acc[:],
                        lhsT=wq[b][:, m].bitcast(FP8X4),
                        lhsT_scale=ws[b][:, m],
                        rhs=vw[a][n][:].bitcast(FP8X4),
                        rhs_scale=vs[4 * a : P, n * BANK : (n + 1) * BANK],
                        start=(a == 0),
                        stop=(a == 1),
                    )
                nc.scalar.activation(out=th[:, n * BANK : (n + 1) * BANK], in_=acc[:], func=ACT.Tanh)
            return th

        def times_gain(s, th):
            b, t = divmod(s, PACK)
            h = slot(s % 4, [P, S], F32, "h")
            if s in GAIN_ON_VECTOR:
                width = BANK if s == 0 else S
                for n0 in range(0, S, width):
                    cols = slice(n0, n0 + width)
                    nc.vector.tensor_scalar(
                        out=h[:, cols], in0=th[:, cols], scalar1=gain_t[:, b, t : t + 1], scalar2=None, op0=ALU.mult
                    )
            else:
                nc.scalar.activation(out=h[:], in_=th[:], func=ACT.Copy, scale=gain_t[:, b, t : t + 1])
            return h

        def pick1(h, s, j0, width, g):
            cols = slice(j0 // 16, (j0 + width) // 16)
            nc.vector.tensor_tensor(g[:, s % PACK, :], h[:].indirect(p1[:, cols]), room_t[s][:, j0 : j0 + width], ALU.mult)

        def pick2(h, s, j0, width, g):
            cols = slice(j0 // 16, (j0 + width) // 16)
            nc.vector.tensor_copy(g[:, s % PACK, :], h[:].indirect(p2[:, cols]))

        def floor_aside(s, g):
            b, t = divmod(s, PACK)
            nc.gpsimd.tensor_scalar(
                out=g[:, t, :],
                in0=g[:, t, :],
                scalar1=F32_MAX,
                scalar2=base_t[:, b, t : t + 1],
                op0=ALU.min,
                op1=ALU.max,
            )

        def floor(s, g):
            b, t = divmod(s, PACK)
            nc.vector.tensor_scalar(
                out=g[:, t, :], in0=g[:, t, :], scalar1=base_t[:, b, t : t + 1], scalar2=None, op0=ALU.max
            )

        def interleaved(xb):
            return xb.rearrange("p (c i t) -> p c t i", i=4, t=PACK)

        def by_rows(g):
            return g.rearrange("p t (c i) -> p c t i", i=4)

        def quantise_x(xb, width, name):
            xq = held([P, width], U32, f"xq{name}")
            xs = held([P, width], U8, f"xs{name}")
            nc.vector.quantize_mx(out=xq[:].bitcast(FP8X4), scales=xs[:], in_=xb)
            return xq, xs

        g0 = [held([P, PACK, J], F32, f"g0{i}") for i in range(2)]

        def picks0(h, s):
            pick2(h, s, 0, J, g0[1])
            pick1(h, s, 0, J, g0[0])
            floor_aside(s, g0[1])

        def second_half_of_w(a):
            wb = held([P, PACK * PASS], BF16, "wb")
            round_w(nc.scalar.copy, wb[:], 1, a, 0, 2)
            quantise_w(wb[:], 1, a * PASS, (a + 1) * PASS)

        h = times_gain(0, first_product(0))
        th = first_product(1)
        picks0(h, 0)
        second_half_of_w(0)
        picks0(times_gain(1, th), 1)
        th = first_product(2)
        second_half_of_w(1)
        h = times_gain(2, th)
        h3 = times_gain(3, first_product(3))
        picks0(h, 2)
        picks0(h3, 3)
        v2w = [held([P, S2], U32, "v2w0"), keep.tile([P, S2], U32, name="v2w1", tag="wb", align_bytes=64)]
        for b in range(2):
            gather(v2w[b][:], tab2w[b], idx2[:])

        hs = [times_gain(s, first_product(s)) for s in range(4, 8)]
        xb0 = keep.tile([P, 2, PACK * J], BF16, name="xb0", tag="th1", align_bytes=64)
        x0 = []
        for i in range(2):
            nc.scalar.copy(out=interleaved(xb0[:, i, :]), in_=by_rows(g0[i][:]))
            x0.append(quantise_x(xb0[:, i, :], J, f"0{i}"))
        x1 = []
        ga = held([P, PACK, J], F32, "ga")
        for c in range(2):
            gb = keep.tile([P, PACK, CHUNK], F32, name="gb", tag=("gb", "th1")[c], align_bytes=64)
            for s in range(4, 8):
                pick2(hs[s - 4], s, c * CHUNK, CHUNK, gb)
                if c == 0:
                    pick1(hs[s - 4], s, 0, J, ga)
            for s in range(4, 8):
                (floor_aside, floor)[c](s, gb)
            xa = held([P, PACK * CHUNK], BF16, f"xa{c}")
            xb = held([P, PACK * CHUNK], BF16, f"xb{c}")
            copy = nc.scalar.copy if c == 0 else nc.vector.tensor_copy
            copy(out=interleaved(xb[:]), in_=by_rows(gb[:]))
            nc.scalar.copy(out=interleaved(xa[:]), in_=by_rows(ga[:, :, c * CHUNK : (c + 1) * CHUNK]))
            x1.append([quantise_x(xa[:], CHUNK, f"1{c}0"), quantise_x(xb[:], CHUNK, f"1{c}1")])

        for c in range(2):
            cols = slice(c * CHUNK, (c + 1) * CHUNK)
            for mp in range(2):
                e = [psum.tile([P, 2, CHUNK], F32, name="acc") for i in range(2)]
                for b in range(2):
                    for i in (1, 0):
                        for u in range(2):
                            m = slice((2 * mp + u) * P, (2 * mp + u + 1) * P)
                            xq, xs = x0[i] if b == 0 else x1[c][i]
                            xcols = cols if b == 0 else slice(0, CHUNK)
                            nc.tensor.matmul_mx(
                                out=e[i][:, u, :],
                                lhsT=v2w[b][:, m].bitcast(FP8X4),
                                lhsT_scale=v2s[4 * b : P, m],
                                rhs=xq[:, xcols].bitcast(FP8X4),
                                rhs_scale=xs[:, xcols],
                                start=(b == 0 and u == 0),
                                stop=(b == 1 and u == 1),
                            )
                e2 = ring.tile([P, 2, CHUNK], F32, name="e2")
                nc.scalar.copy(out=e2[:], in_=e[1][:])
                prod = ring.tile([P, 2, CHUNK], F32, name="prod")
                for u in range(2):
                    nc.vector.tensor_tensor(prod[:, u, :], e[0][:, u, :], e2[:, u, :], ALU.mult)
                res = ring.tile([P, 2, CHUNK], F32, name="res")
                for u in range(2):
                    mt = 2 * mp + u
                    nc.vector.scalar_tensor_tensor(
                        out=res[:, u, :],
                        in0=e[0][:, u, :],
                        scalar=level_t[:, mt : mt + 1],
                        in1=prod[:, u, :],
                        op0=ALU.max,
                        op1=ALU.add,
                    )
                    nc.sync.dma_start(out=out[mt * P : (mt + 1) * P, cols], in_=res[:, u, :])
